import numpy as np
import ml_dtypes


def mxq(x, axis, fmt="e4m3"):
    dtype, down = {"e4m3": (ml_dtypes.float8_e4m3fn, 7), "e5m2": (ml_dtypes.float8_e5m2, 14)}[fmt]
    v = np.moveaxis(np.asarray(x, np.float32).astype(ml_dtypes.bfloat16).astype(np.float64), axis, -1)
    blocks = v.reshape(v.shape[:-1] + (-1, 32))
    amax = np.abs(blocks).max(-1, keepdims=True)
    byte = np.maximum(np.where(amax > 0, np.frexp(amax)[1] - 1 + 127, 0) - down, 1)
    scale = np.exp2(byte - 127.0)
    codes = (blocks / scale).astype(np.float32).astype(dtype).astype(np.float64)
    return np.moveaxis((codes * scale).reshape(v.shape), -1, axis)


WIDE = False


def mx_kscale(k):
    if not WIDE:
        return np.ones(k)
    levels = np.array([10, -10, 5, -5, 0])
    if k % 512:
        return np.exp2(np.random.permutation(np.resize(levels, k // 32))).repeat(32)
    a = np.empty((k // 512, 16))
    for p in range(k // 512):
        a[p, :8] = np.random.permutation(np.resize(levels, 8))
        for g in range(8):
            far = levels[np.abs(levels - a[p, g]) >= 10]
            a[p, g + 8] = far[np.random.randint(len(far))]
    return np.exp2(a.ravel()).repeat(32)


BF16 = ml_dtypes.bfloat16


def bf(x):
    return np.asarray(x, np.float32).astype(BF16)


def f64(x):
    return np.asarray(x).astype(np.float64)

E4M3FN = np.array([(-1.0 if i & 128 else 1.0) * ((1.0 + (i & 7) / 8.0) * 2.0 ** (((i >> 3) & 15) - 7) if i & 120 else (i & 7) * 2.0 ** -9) for i in range(256)])


def e4m3fn_bytes(y):
    return np.clip(np.asarray(y, np.float64), -448.0, 448.0).astype(np.float32).astype(ml_dtypes.float8_e4m3fn).view(np.uint8)


def e4m3fn_values(b):
    return E4M3FN[b]


T, K, V, C, B = 1024, 1024, 1024, 3, 128
FP8_MAX = 448.0


def setup_inputs():
    s = mx_kscale(K)
    a = np.random.uniform(0.0, 1.0, (T, K)) * s
    d = np.random.standard_normal((K, V * C)) * np.sqrt(C / K) / s[:, None]
    a_scale = (np.abs(a).reshape(T, K // B, B).max(axis=2) / FP8_MAX).astype(np.float32)
    d_scale = (np.abs(d).reshape(K // B, B, V * C // B, B).max(axis=(1, 3)) / FP8_MAX).astype(np.float32)
    return {"A_bytes": e4m3fn_bytes(a / np.repeat(f64(a_scale), B, axis=1)),
            "A_scale": a_scale,
            "D_bytes": e4m3fn_bytes(d / np.repeat(np.repeat(f64(d_scale), B, axis=0), B, axis=1)),
            "D_scale": d_scale,
            "neutral": bf(np.random.standard_normal((V, C))),
            "strength": bf(1 + 0.1 * np.random.standard_normal(V)),
            "shift": bf(0.3 * np.random.standard_normal((T, C)))}


def reference(A_bytes, A_scale, D_bytes, D_scale, neutral, strength, shift):
    A = e4m3fn_values(A_bytes) * np.repeat(f64(A_scale), B, axis=1)
    D = e4m3fn_values(D_bytes) * np.repeat(np.repeat(f64(D_scale), B, axis=0), B, axis=1)
    delta = (mxq(A, 1, "e4m3") @ mxq(D, 0, "e4m3")).reshape(T, V, C)
    return delta * f64(strength)[:, None] + f64(neutral) + f64(shift)[:, None, :]

@@ -1,0 +1,268 @@
+from contextlib import ExitStack
+
+import concourse.mybir as mybir
+from concourse.masks import make_identity
+
+FRAMES, K, VERTS, COORDS, SCALE_BLOCK = 1024, 1024, 1024, 3, 128
+COLS = VERTS * COORDS
+FLOPS = 2 * FRAMES * K * COLS
+
+F32 = mybir.dt.float32
+BF16 = mybir.dt.bfloat16
+U32 = mybir.dt.uint32
+U8 = mybir.dt.uint8
+F8 = mybir.dt.float8_e4m3fn
+FP8X4 = mybir.dt.float8_e4m3fn_x4
+MULT = mybir.AluOpType.mult
+ADD = mybir.AluOpType.add
+COPY = mybir.ActivationFunctionType.Copy
+IDENTITY = mybir.ActivationFunctionType.Identity
+
+P = 128
+PASSES = K // 512
+TILES = FRAMES // P
+HALF = TILES // 2
+GROUP = P * COORDS
+GROUPS = COLS // GROUP
+S_A = (2, 5, 7)
+
+
+def tile_blendshape_face_rig_d2_kernel(tc, A_bytes, A_scale, D_bytes, D_scale, neutral, strength, shift, out):
+    nc = tc.nc
+    with ExitStack() as ctx:
+        keep = ctx.enter_context(tc.tile_pool(name="keep", bufs=1))
+        work = ctx.enter_context(tc.tile_pool(name="work", bufs=4))
+        psum = ctx.enter_context(tc.psum_pool(name="psum", bufs=4))
+        ctx.enter_context(tc.manual_schedule())
+
+        a_sc = keep.tile([P, TILES, K // SCALE_BLOCK], F32, name="a_sc")
+        nc.sync.dma_start(out=a_sc[:], in_=A_scale.rearrange("(p i) j -> p i j", i=TILES))
+        a_view = A_bytes.rearrange("(p i) k -> p i k", i=TILES)
+        d_view = D_bytes.rearrange("(g p t) n -> g p t n", p=P, t=4)
+        a_by = []
+        d_by = {}
+
+        def load_a(pair):
+            t = keep.tile([P, 2, K], U8, name="a_by%d" % pair)
+            nc.sync.dma_start(out=t[:], in_=a_view[:, 2 * pair : 2 * pair + 2, :])
+            a_by.append(t)
+
+        def load_d(s, g):
+            t = keep.tile([P, 4, GROUP], U8, name="d_by%d_%d" % (s, g))
+            nc.sync.dma_start(out=t[:], in_=d_view[g][:, :, s * GROUP : (s + 1) * GROUP])
+            d_by[s, g] = t
+
+        load_a(0)
+        load_a(1)
+        for g in range(PASSES):
+            load_d(0, g)
+        load_a(2)
+        load_a(3)
+        for s in range(1, GROUPS):
+            for g in range(PASSES):
+                load_d(s, g)
+
+        d_sc = keep.tile([P, PASSES, COLS // SCALE_BLOCK], F32, name="d_sc")
+        d_sc_view = D_scale.rearrange("(g q) j -> q g j", q=4)
+        for q in range(4):
+            nc.scalar.dma_start(out=d_sc[32 * q : 32 * q + 32, :, :], in_=d_sc_view[q].partition_broadcast(32))
+        nb = keep.tile([8, GROUP], BF16, name="nb")
+        nc.gpsimd.dma_start(out=nb[:], in_=neutral.rearrange("(r v) c -> r (v c)", r=8))
+        stb = keep.tile([P, P], BF16, name="stb")
+        nc.gpsimd.dma_start(out=stb[32:40, :], in_=strength.rearrange("(r v) -> r v", r=8))
+        shb = keep.tile([P, TILES * COORDS], BF16, name="shb")
+        nc.gpsimd.dma_start(out=shb[:], in_=shift.rearrange("(p i) c -> p (i c)", i=TILES))
+
+        ident = keep.tile([P, P], F32, name="ident")
+        make_identity(nc, ident[:])
+        ns = keep.tile([P, GROUP], F32, name="ns")
+        nc.gpsimd.memset(ns[:], 0.0)
+
+        a_codes = keep.tile([P, PASSES, FRAMES], U32, name="a_codes", align_bytes=64)
+        a_scales = keep.tile([P, PASSES, FRAMES], U8, name="a_scales", align_bytes=64)
+        d_codes = keep.tile([P, COLS // P, PASSES * P], U32, name="d_codes", align_bytes=64)
+        d_scales = keep.tile([P, COLS // P, PASSES * P], U8, name="d_scales", align_bytes=64)
+
+        a_bf = {}
+
+        def a_widen(i):
+            pair, ii = divmod(i, 2)
+            if ii == 0:
+                a_bf[pair] = keep.tile([P, 2, K], BF16, name="a_bf%d" % pair)
+            for j in range(K // SCALE_BLOCK):
+                cols = slice(SCALE_BLOCK * j, SCALE_BLOCK * (j + 1))
+                src = a_by[pair][:, ii, cols].bitcast(F8)
+                dst = a_bf[pair][:, ii, cols]
+                if j in S_A:
+                    nc.scalar.activation(out=dst, in_=src, func=COPY, scale=a_sc[:, i, j : j + 1])
+                else:
+                    nc.vector.tensor_scalar(out=dst, in0=src, scalar1=a_sc[:, i, j : j + 1], scalar2=None, op0=MULT)
+
+        a_grp = {}
+
+        def a_turn(pair, g, copy):
+            h, part = divmod(pair, 2)
+            if part == 0:
+                a_grp[h, g] = work.tile([P, HALF * P * 4], BF16, name="a_grp", align_bytes=64)
+            bank = psum.tile([P, 512], F32, name="tr")
+            for ii in range(2):
+                words = a_bf[pair][:, ii, :].bitcast(F32)
+                for u in range(2):
+                    at = 256 * ii + 128 * u
+                    nc.tensor.transpose(bank[:, at : at + 128], words[:, 256 * g + u : 256 * (g + 1) : 2], ident[:])
+            dst = a_grp[h, g][:].bitcast(F32)[:, 512 * part : 512 * (part + 1)].rearrange("p (i r u) -> p i r u", i=2, u=2)
+            copy(out=dst, in_=bank[:].rearrange("p (i u r) -> p i r u", i=2, u=2))
+
+        def a_quant(h, g):
+            f = slice(512 * h, 512 * (h + 1))
+            nc.vector.quantize_mx(out=a_codes[:, g, f].bitcast(FP8X4), scales=a_scales[:, g, f], in_=a_grp[h, g][:])
+
+        d_wd = {}
+        d_il = {}
+
+        def d_widen(s, g, part):
+            if part == 0:
+                d_wd[s, g] = work.tile([P, 4 * GROUP], BF16, name="d_wd", bufs=6)
+            cols = slice(768 * part, 768 * (part + 1))
+            nc.scalar.copy(out=d_wd[s, g][:, cols], in_=d_by[s, g][:].rearrange("p t n -> p (t n)")[:, cols].bitcast(F8))
+
+        def d_inter(jt, g):
+            s, j = divmod(jt, COORDS)
+            if g == 0:
+                d_il[jt] = work.tile([P, PASSES * P * 4], BF16, name="d_il", align_bytes=64)
+            src = d_wd[s, g][:].rearrange("p (t n) -> p n t", t=4)[:, P * j : P * (j + 1), :]
+            dst = d_il[jt][:, 512 * g : 512 * (g + 1)].rearrange("p (n t) -> p n t", t=4)
+            nc.vector.tensor_scalar(out=dst, in0=src, scalar1=d_sc[:, g, jt : jt + 1], scalar2=None, op0=MULT)
+
+        def d_quant(jt):
+            nc.vector.quantize_mx(out=d_codes[:, jt, :].bitcast(FP8X4), scales=d_scales[:, jt, :], in_=d_il[jt][:])
+
+        nsv = keep.tile([P, COORDS, 40], F32, name="nsv")
+        x = {}
+
+        def product(u, j):
+            s, h = divmod(u, 2)
+            jt = COORDS * s + j
+            f = slice(512 * h, 512 * (h + 1))
+            bank = psum.tile([P, 512], F32, name="mx")
+            for g in range(PASSES):
+                c = slice(P * g, P * (g + 1))
+                nc.tensor.matmul_mx(
+                    out=bank[:],
+                    lhsT=d_codes[:, jt, c].bitcast(FP8X4), lhsT_scale=d_scales[:, jt, c],
+                    rhs=a_codes[:, g, f].bitcast(FP8X4), rhs_scale=a_scales[:, g, f],
+                    start=(g == 0), stop=(g == PASSES - 1),
+                )
+            x[u, j] = work.tile([P, 512], F32, name="x", bufs=8)
+            nc.scalar.activation(out=x[u, j][:], in_=bank[:], func=IDENTITY, scale=nsv[:, j, 32 + s : 33 + s], bias=nsv[:, j, s : s + 1])
+
+        turned = {}
+
+        def turn(u, ii):
+            bank = psum.tile([P, 512], F32, name="tr")
+            for j in range(COORDS):
+                nc.tensor.transpose(bank[:, P * j : P * (j + 1)], x[u, j][:, P * ii : P * (ii + 1)], ident[:])
+            turned[u, ii] = bank
+
+        out_view = out.rearrange("(p i) v c -> p i (v c)", i=TILES)
+        o = {}
+
+        def shifted(u, ii, single):
+            s, h = divmod(u, 2)
+            i = HALF * h + ii
+            if ii % 2 == 0:
+                o[u, ii // 2] = work.tile([P, 2, GROUP], F32, name="o", bufs=6)
+            t = o[u, ii // 2]
+            nc.vector.tensor_tensor(
+                out=t[:, ii % 2, :].rearrange("p (v c) -> p v c", c=COORDS),
+                in0=turned[u, ii][:, 0:GROUP].rearrange("p (v c) -> p v c", c=COORDS),
+                in1=shb[:, COORDS * i : COORDS * (i + 1)].unsqueeze(1).to_broadcast([P, P, COORDS]),
+                op=ADD,
+            )
+            cols = slice(GROUP * s, GROUP * (s + 1))
+            if single:
+                nc.sync.dma_start(out=out_view[:, i, cols], in_=t[:, ii % 2, :])
+            elif ii % 2 == 1:
+                nc.sync.dma_start(out=out_view[:, i - 1 : i + 1, cols], in_=t[:])
+
+        a_widen(0)
+        a_widen(1)
+        a_turn(0, 0, nc.scalar.copy)
+        a_turn(0, 1, nc.vector.tensor_copy)
+        a_widen(2)
+        a_widen(3)
+        for part in range(2):
+            d_widen(0, 0, part)
+        a_turn(1, 0, nc.scalar.copy)
+        a_turn(1, 1, nc.vector.tensor_copy)
+        for part in range(2):
+            d_widen(0, 1, part)
+        a_quant(0, 0)
+        d_inter(0, 0)
+        a_quant(0, 1)
+        d_inter(0, 1)
+        nc.vector.tensor_copy(out=ns[0:8, :], in_=nb[:])
+        nc.vector.tensor_copy(out=ns[32:40, :].rearrange("p (v c) -> p v c", c=COORDS), in_=stb[32:40, :].unsqueeze(2).to_broadcast([8, P, COORDS]))
+        bank = psum.tile([P, 512], F32, name="tr")
+        for j in range(COORDS):
+            nc.tensor.transpose(bank[:, P * j : P * (j + 1)], ns[:, P * j : P * (j + 1)], ident[:])
+        d_quant(0)
+        nc.vector.tensor_copy(out=nsv[:], in_=bank[:, 0:GROUP].rearrange("p (j r) -> p j r", j=COORDS)[:, :, 0:40])
+        product(0, 0)
+        for jt in (1, 2):
+            d_inter(jt, 0)
+            d_inter(jt, 1)
+            d_quant(jt)
+            product(0, jt)
+        a_widen(4)
+        a_widen(5)
+        a_turn(2, 0, nc.scalar.copy)
+        a_turn(2, 1, nc.vector.tensor_copy)
+        a_widen(6)
+        a_widen(7)
+        a_turn(3, 0, nc.scalar.copy)
+        a_turn(3, 1, nc.vector.tensor_copy)
+        a_quant(1, 0)
+        a_quant(1, 1)
+
+        widens = [(s, g, part) for s in range(1, GROUPS) for g in range(PASSES) for part in range(2)]
+        preps = []
+        last = None
+        for jt in range(COORDS, COLS // P):
+            preps.append((d_inter, (jt, 0)))
+            if last is not None:
+                preps.append((d_quant, (last,)))
+            preps.append((d_inter, (jt, 1)))
+            last = jt
+        preps.append((d_quant, (last,)))
+
+        def widen_next(n):
+            for w in widens[:n]:
+                d_widen(*w)
+            rest = widens[n:]
+            widens.clear()
+            widens.extend(rest)
+
+        def prep_next(n):
+            for f, args in preps[:n]:
+                f(*args)
+            rest = preps[n:]
+            preps.clear()
+            preps.extend(rest)
+
+        units = 2 * GROUPS
+        widen_next(4)
+        prep_next(2)
+        for u in range(units + 1):
+            for step in range(4):
+                if 0 < u < units and step < COORDS:
+                    product(u, step)
+                if step in (0, 2):
+                    widen_next(1)
+                if step == 3 and u >= 1:
+                    for ii in range(4):
+                        turn(u - 1, ii)
+            for step in range(4):
+                if u >= 1:
+                    shifted(u - 1, step, u == units)
+                prep_next(2 if step == 0 and u % 2 == 0 else 1)

@@ -24,11 +24,15 @@ TILES = FRAMES // P
 HALF = TILES // 2
 GROUP = P * COORDS
 GROUPS = COLS // GROUP
+W_LEAD, P_LEAD = 2, 5
+V_WIDEN = (1, 9, 11, 14, 17, 19, 22, 25, 27, 30)
+S_OUT, S_OUT_UNITS = (3,), 11
 S_A = (2, 5, 7)
 
 
 def tile_blendshape_face_rig_d2_kernel(tc, A_bytes, A_scale, D_bytes, D_scale, neutral, strength, shift, out):
     nc = tc.nc
+    VC, SC = nc.vector.tensor_copy, nc.scalar.copy
     with ExitStack() as ctx:
         keep = ctx.enter_context(tc.tile_pool(name="keep", bufs=1))
         work = ctx.enter_context(tc.tile_pool(name="work", bufs=4))
@@ -66,22 +70,35 @@ def tile_blendshape_face_rig_d2_kernel(tc, A_bytes, A_scale, D_bytes, D_scale, n
         d_sc_view = D_scale.rearrange("(g q) j -> q g j", q=4)
         for q in range(4):
             nc.scalar.dma_start(out=d_sc[32 * q : 32 * q + 32, :, :], in_=d_sc_view[q].partition_broadcast(32))
-        nb = keep.tile([8, GROUP], BF16, name="nb")
-        nc.gpsimd.dma_start(out=nb[:], in_=neutral.rearrange("(r v) c -> r (v c)", r=8))
         stb = keep.tile([P, P], BF16, name="stb")
-        nc.gpsimd.dma_start(out=stb[32:40, :], in_=strength.rearrange("(r v) -> r v", r=8))
-        shb = keep.tile([P, TILES * COORDS], BF16, name="shb")
-        nc.gpsimd.dma_start(out=shb[:], in_=shift.rearrange("(p i) c -> p (i c)", i=TILES))
-
+        nc.scalar.dma_start(out=stb[32:40, :], in_=strength.rearrange("(r v) -> r v", r=8))
         ident = keep.tile([P, P], F32, name="ident")
         make_identity(nc, ident[:])
-        ns = keep.tile([P, GROUP], F32, name="ns")
+        ns = keep.tile([P, GROUP], BF16, name="ns")
         nc.gpsimd.memset(ns[:], 0.0)
+        sh = keep.tile([P, P], BF16, name="sh")
+        nc.gpsimd.memset(sh[:], 0.0)
+        ident_bf = keep.tile([P, P], BF16, name="ident_bf")
+        make_identity(nc, ident_bf[:])
+        nc.scalar.dma_start(out=ns[0:8, :], in_=neutral.rearrange("(r v) c -> r (v c)", r=8))
+        nc.scalar.dma_start(out=sh[:, 0 : TILES * COORDS], in_=shift.rearrange("(p i) c -> p (i c)", i=TILES))
+        nc.gpsimd.tensor_copy(out=ns[32:40, :].rearrange("p (v c) -> p v c", c=COORDS), in_=stb[32:40, :].unsqueeze(2).to_broadcast([8, P, COORDS]))
 
         a_codes = keep.tile([P, PASSES, FRAMES], U32, name="a_codes", align_bytes=64)
         a_scales = keep.tile([P, PASSES, FRAMES], U8, name="a_scales", align_bytes=64)
         d_codes = keep.tile([P, COLS // P, PASSES * P], U32, name="d_codes", align_bytes=64)
         d_scales = keep.tile([P, COLS // P, PASSES * P], U8, name="d_scales", align_bytes=64)
+
+        sh_t = keep.tile([P, P], BF16, name="sh_t")
+        nsv = keep.tile([P, COORDS, 40], F32, name="nsv")
+
+        def small_turns():
+            bank = psum.tile([P, 1024], BF16, name="tr")
+            for j in range(COORDS):
+                nc.tensor.transpose(bank[:, P * j : P * (j + 1)], ns[:, P * j : P * (j + 1)], ident_bf[:])
+            nc.tensor.transpose(bank[:, GROUP : GROUP + P], sh[:], ident_bf[:])
+            nc.vector.tensor_copy(out=nsv[:], in_=bank[:, 0:GROUP].rearrange("p (j r) -> p j r", j=COORDS)[:, :, 0:40])
+            nc.vector.tensor_copy(out=sh_t[:], in_=bank[:, GROUP : GROUP + P])
 
         a_bf = {}
 
@@ -100,16 +117,22 @@ def tile_blendshape_face_rig_d2_kernel(tc, A_bytes, A_scale, D_bytes, D_scale, n
 
         a_grp = {}
 
-        def a_turn(pair, g, copy):
-            h, part = divmod(pair, 2)
-            if part == 0:
-                a_grp[h, g] = work.tile([P, HALF * P * 4], BF16, name="a_grp", align_bytes=64)
+        a_bank = {}
+
+        def a_turn(pair, g):
             bank = psum.tile([P, 512], F32, name="tr")
             for ii in range(2):
                 words = a_bf[pair][:, ii, :].bitcast(F32)
                 for u in range(2):
                     at = 256 * ii + 128 * u
                     nc.tensor.transpose(bank[:, at : at + 128], words[:, 256 * g + u : 256 * (g + 1) : 2], ident[:])
+            a_bank[pair, g] = bank
+
+        def a_out(pair, g, copy):
+            h, part = divmod(pair, 2)
+            bank = a_bank[pair, g]
+            if part == 0:
+                a_grp[h, g] = work.tile([P, HALF * P * 4], BF16, name="a_grp", align_bytes=64)
             dst = a_grp[h, g][:].bitcast(F32)[:, 512 * part : 512 * (part + 1)].rearrange("p (i r u) -> p i r u", i=2, u=2)
             copy(out=dst, in_=bank[:].rearrange("p (i u r) -> p i r u", i=2, u=2))
 
@@ -124,7 +147,8 @@ def tile_blendshape_face_rig_d2_kernel(tc, A_bytes, A_scale, D_bytes, D_scale, n
             if part == 0:
                 d_wd[s, g] = work.tile([P, 4 * GROUP], BF16, name="d_wd", bufs=6)
             cols = slice(768 * part, 768 * (part + 1))
-            nc.scalar.copy(out=d_wd[s, g][:, cols], in_=d_by[s, g][:].rearrange("p t n -> p (t n)")[:, cols].bitcast(F8))
+            copy = VC if (4 * s + 2 * g + part) % 32 in V_WIDEN else SC
+            copy(out=d_wd[s, g][:, cols], in_=d_by[s, g][:].rearrange("p t n -> p (t n)")[:, cols].bitcast(F8))
 
         def d_inter(jt, g):
             s, j = divmod(jt, COORDS)
@@ -137,7 +161,6 @@ def tile_blendshape_face_rig_d2_kernel(tc, A_bytes, A_scale, D_bytes, D_scale, n
         def d_quant(jt):
             nc.vector.quantize_mx(out=d_codes[:, jt, :].bitcast(FP8X4), scales=d_scales[:, jt, :], in_=d_il[jt][:])
 
-        nsv = keep.tile([P, COORDS, 40], F32, name="nsv")
         x = {}
 
         def product(u, j):
@@ -158,10 +181,24 @@ def tile_blendshape_face_rig_d2_kernel(tc, A_bytes, A_scale, D_bytes, D_scale, n
 
         turned = {}
 
+        def s_out(u):
+            return S_OUT if u < S_OUT_UNITS else ()
+
         def turn(u, ii):
             bank = psum.tile([P, 512], F32, name="tr")
+            i = HALF * (u % 2) + ii
+            if ii in s_out(u):
+                nc.tensor.matmul(
+                    bank[:, 0:GROUP].rearrange("p (v c) -> p v c", c=COORDS), lhsT=sh_t[:],
+                    rhs=ident_bf[:, COORDS * i : COORDS * (i + 1)].unsqueeze(1).to_broadcast([P, P, COORDS]),
+                    start=True, stop=False,
+                )
             for j in range(COORDS):
-                nc.tensor.transpose(bank[:, P * j : P * (j + 1)], x[u, j][:, P * ii : P * (ii + 1)], ident[:])
+                block, src = bank[:, P * j : P * (j + 1)], x[u, j][:, P * ii : P * (ii + 1)]
+                if ii in s_out(u):
+                    nc.tensor.matmul(block, lhsT=src, rhs=ident[:], start=False, stop=(j == COORDS - 1), is_transpose=True)
+                else:
+                    nc.tensor.transpose(block, src, ident[:])
             turned[u, ii] = bank
 
         out_view = out.rearrange("(p i) v c -> p i (v c)", i=TILES)
@@ -173,10 +210,13 @@ def tile_blendshape_face_rig_d2_kernel(tc, A_bytes, A_scale, D_bytes, D_scale, n
             if ii % 2 == 0:
                 o[u, ii // 2] = work.tile([P, 2, GROUP], F32, name="o", bufs=6)
             t = o[u, ii // 2]
-            nc.vector.tensor_tensor(
+            if ii in s_out(u):
+                nc.scalar.copy(out=t[:, ii % 2, :], in_=turned[u, ii][:, 0:GROUP])
+            else:
+              nc.vector.tensor_tensor(
                 out=t[:, ii % 2, :].rearrange("p (v c) -> p v c", c=COORDS),
                 in0=turned[u, ii][:, 0:GROUP].rearrange("p (v c) -> p v c", c=COORDS),
-                in1=shb[:, COORDS * i : COORDS * (i + 1)].unsqueeze(1).to_broadcast([P, P, COORDS]),
+                in1=sh[:, COORDS * i : COORDS * (i + 1)].unsqueeze(1).to_broadcast([P, P, COORDS]),
                 op=ADD,
             )
             cols = slice(GROUP * s, GROUP * (s + 1))
@@ -185,47 +225,52 @@ def tile_blendshape_face_rig_d2_kernel(tc, A_bytes, A_scale, D_bytes, D_scale, n
             elif ii % 2 == 1:
                 nc.sync.dma_start(out=out_view[:, i - 1 : i + 1, cols], in_=t[:])
 
-        a_widen(0)
-        a_widen(1)
-        a_turn(0, 0, nc.scalar.copy)
-        a_turn(0, 1, nc.vector.tensor_copy)
-        a_widen(2)
-        a_widen(3)
-        for part in range(2):
-            d_widen(0, 0, part)
-        a_turn(1, 0, nc.scalar.copy)
-        a_turn(1, 1, nc.vector.tensor_copy)
+        for i in range(HALF):
+            a_widen(i)
+        for pair in (0, 1):
+            for g in range(PASSES):
+                a_turn(pair, g)
+        d_widen(0, 0, 0)
+        a_out(0, 0, VC)
+        a_out(0, 1, VC)
+        d_widen(0, 0, 1)
+        a_out(1, 0, VC)
+        a_out(1, 1, SC)
+        d_inter(0, 0)
+        a_quant(0, 0)
         for part in range(2):
             d_widen(0, 1, part)
-        a_quant(0, 0)
-        d_inter(0, 0)
         a_quant(0, 1)
+        small_turns()
         d_inter(0, 1)
-        nc.vector.tensor_copy(out=ns[0:8, :], in_=nb[:])
-        nc.vector.tensor_copy(out=ns[32:40, :].rearrange("p (v c) -> p v c", c=COORDS), in_=stb[32:40, :].unsqueeze(2).to_broadcast([8, P, COORDS]))
-        bank = psum.tile([P, 512], F32, name="tr")
-        for j in range(COORDS):
-            nc.tensor.transpose(bank[:, P * j : P * (j + 1)], ns[:, P * j : P * (j + 1)], ident[:])
+        for i in range(HALF, TILES):
+            a_widen(i)
+        a_turn(2, 0)
+        a_turn(2, 1)
         d_quant(0)
-        nc.vector.tensor_copy(out=nsv[:], in_=bank[:, 0:GROUP].rearrange("p (j r) -> p j r", j=COORDS)[:, :, 0:40])
+        d_widen(1, 0, 0)
+        d_widen(1, 0, 1)
         product(0, 0)
-        for jt in (1, 2):
-            d_inter(jt, 0)
-            d_inter(jt, 1)
-            d_quant(jt)
-            product(0, jt)
-        a_widen(4)
-        a_widen(5)
-        a_turn(2, 0, nc.scalar.copy)
-        a_turn(2, 1, nc.vector.tensor_copy)
-        a_widen(6)
-        a_widen(7)
-        a_turn(3, 0, nc.scalar.copy)
-        a_turn(3, 1, nc.vector.tensor_copy)
+        d_inter(1, 0)
+        a_turn(3, 0)
+        a_turn(3, 1)
+        d_inter(1, 1)
+        a_out(2, 0, VC)
+        d_quant(1)
+        a_out(2, 1, SC)
+        a_out(3, 0, VC)
+        product(0, 1)
+        d_inter(2, 0)
+        d_inter(2, 1)
         a_quant(1, 0)
+        d_quant(2)
+        a_out(3, 1, SC)
+        d_widen(1, 1, 0)
+        d_widen(1, 1, 1)
+        product(0, 2)
         a_quant(1, 1)
 
-        widens = [(s, g, part) for s in range(1, GROUPS) for g in range(PASSES) for part in range(2)]
+        widens = [(s, g, part) for s in range(2, GROUPS) for g in range(PASSES) for part in range(2)]
         preps = []
         last = None
         for jt in range(COORDS, COLS // P):
@@ -251,8 +296,8 @@ def tile_blendshape_face_rig_d2_kernel(tc, A_bytes, A_scale, D_bytes, D_scale, n
             preps.extend(rest)
 
         units = 2 * GROUPS
-        widen_next(4)
-        prep_next(2)
+        widen_next(W_LEAD)
+        prep_next(P_LEAD)
         for u in range(units + 1):
             for step in range(4):
                 if 0 < u < units and step < COORDS:

@@ -72,6 +72,10 @@ def tile_blendshape_face_rig_d2_kernel(tc, A_bytes, A_scale, D_bytes, D_scale, n
             nc.scalar.dma_start(out=d_sc[32 * q : 32 * q + 32, :, :], in_=d_sc_view[q].partition_broadcast(32))
         stb = keep.tile([P, P], BF16, name="stb")
         nc.scalar.dma_start(out=stb[32:40, :], in_=strength.rearrange("(r v) -> r v", r=8))
+        nb = keep.tile([8, GROUP], BF16, name="nb")
+        nc.scalar.dma_start(out=nb[:], in_=neutral.rearrange("(r v) c -> r (v c)", r=8))
+        shb = keep.tile([P, TILES * COORDS], BF16, name="shb")
+        nc.scalar.dma_start(out=shb[:], in_=shift.rearrange("(p i) c -> p (i c)", i=TILES))
         ident = keep.tile([P, P], F32, name="ident")
         make_identity(nc, ident[:])
         ns = keep.tile([P, GROUP], BF16, name="ns")
@@ -80,8 +84,8 @@ def tile_blendshape_face_rig_d2_kernel(tc, A_bytes, A_scale, D_bytes, D_scale, n
         nc.gpsimd.memset(sh[:], 0.0)
         ident_bf = keep.tile([P, P], BF16, name="ident_bf")
         make_identity(nc, ident_bf[:])
-        nc.scalar.dma_start(out=ns[0:8, :], in_=neutral.rearrange("(r v) c -> r (v c)", r=8))
-        nc.scalar.dma_start(out=sh[:, 0 : TILES * COORDS], in_=shift.rearrange("(p i) c -> p (i c)", i=TILES))
+        nc.gpsimd.tensor_copy(out=ns[0:8, :], in_=nb[:])
+        nc.gpsimd.tensor_copy(out=sh[:, 0 : TILES * COORDS], in_=shb[:])
         nc.gpsimd.tensor_copy(out=ns[32:40, :].rearrange("p (v c) -> p v c", c=COORDS), in_=stb[32:40, :].unsqueeze(2).to_broadcast([8, P, COORDS]))
 
         a_codes = keep.tile([P, PASSES, FRAMES], U32, name="a_codes", align_bytes=64)
@@ -154,8 +158,8 @@ def tile_blendshape_face_rig_d2_kernel(tc, A_bytes, A_scale, D_bytes, D_scale, n
             s, j = divmod(jt, COORDS)
             if g == 0:
                 d_il[jt] = work.tile([P, PASSES * P * 4], BF16, name="d_il", align_bytes=64)
-            src = d_wd[s, g][:].rearrange("p (t n) -> p n t", t=4)[:, P * j : P * (j + 1), :]
-            dst = d_il[jt][:, 512 * g : 512 * (g + 1)].rearrange("p (n t) -> p n t", t=4)
+            src = d_wd[s, g][:].rearrange("p (t n) -> p t n", t=4)[:, :, P * j : P * (j + 1)].rearrange("p t (n i) -> p n t i", i=4)
+            dst = d_il[jt][:, 512 * g : 512 * (g + 1)].rearrange("p (n i t) -> p n t i", i=4, t=4)
             nc.vector.tensor_scalar(out=dst, in0=src, scalar1=d_sc[:, g, jt : jt + 1], scalar2=None, op0=MULT)
 
         def d_quant(jt):
@@ -241,13 +245,13 @@ def tile_blendshape_face_rig_d2_kernel(tc, A_bytes, A_scale, D_bytes, D_scale, n
         for part in range(2):
             d_widen(0, 1, part)
         a_quant(0, 1)
-        small_turns()
         d_inter(0, 1)
         for i in range(HALF, TILES):
             a_widen(i)
         a_turn(2, 0)
         a_turn(2, 1)
         d_quant(0)
+        small_turns()
         d_widen(1, 0, 0)
         d_widen(1, 0, 1)
         product(0, 0)

@@ -24,7 +24,7 @@ TILES = FRAMES // P
 HALF = TILES // 2
 GROUP = P * COORDS
 GROUPS = COLS // GROUP
-W_LEAD, P_LEAD = 2, 5
+W_LEAD, P_LEAD = 2, 4
 V_WIDEN = (1, 9, 11, 14, 17, 19, 22, 25, 27, 30)
 S_OUT, S_OUT_UNITS = (3,), 11
 S_A = (2, 5, 7)
@@ -39,6 +39,14 @@ def tile_blendshape_face_rig_d2_kernel(tc, A_bytes, A_scale, D_bytes, D_scale, n
         psum = ctx.enter_context(tc.psum_pool(name="psum", bufs=4))
         ctx.enter_context(tc.manual_schedule())
 
+        warm = keep.tile([P, 512], BF16, name="warm")
+        nc.vector.memset(warm[:], 0.0)
+
+        def dummies(n):
+            bank = psum.tile([P, 512], F32, name="mx")
+            for again in range(n):
+                nc.tensor.matmul(bank[:], lhsT=warm[:, 0:P], rhs=warm[:], start=True, stop=True)
+
         a_sc = keep.tile([P, TILES, K // SCALE_BLOCK], F32, name="a_sc")
         nc.sync.dma_start(out=a_sc[:], in_=A_scale.rearrange("(p i) j -> p i j", i=TILES))
         a_view = A_bytes.rearrange("(p i) k -> p i k", i=TILES)
@@ -46,22 +54,24 @@ def tile_blendshape_face_rig_d2_kernel(tc, A_bytes, A_scale, D_bytes, D_scale, n
         a_by = []
         d_by = {}
 
-        def load_a(pair):
-            t = keep.tile([P, 2, K], U8, name="a_by%d" % pair)
-            nc.sync.dma_start(out=t[:], in_=a_view[:, 2 * pair : 2 * pair + 2, :])
-            a_by.append(t)
+        def load_a(first, count):
+            t = keep.tile([P, count, K], U8, name="a_by%d" % first)
+            nc.sync.dma_start(out=t[:], in_=a_view[:, first : first + count, :])
+            for i in range(count):
+                a_by.append(t[:, i, :])
 
         def load_d(s, g):
             t = keep.tile([P, 4, GROUP], U8, name="d_by%d_%d" % (s, g))
             nc.sync.dma_start(out=t[:], in_=d_view[g][:, :, s * GROUP : (s + 1) * GROUP])
             d_by[s, g] = t
 
-        load_a(0)
-        load_a(1)
+        load_a(0, 1)
+        load_a(1, 1)
+        load_a(2, 2)
         for g in range(PASSES):
             load_d(0, g)
-        load_a(2)
-        load_a(3)
+        load_a(4, 2)
+        load_a(6, 2)
         for s in range(1, GROUPS):
             for g in range(PASSES):
                 load_d(s, g)
@@ -101,8 +111,8 @@ def tile_blendshape_face_rig_d2_kernel(tc, A_bytes, A_scale, D_bytes, D_scale, n
             for j in range(COORDS):
                 nc.tensor.transpose(bank[:, P * j : P * (j + 1)], ns[:, P * j : P * (j + 1)], ident_bf[:])
             nc.tensor.transpose(bank[:, GROUP : GROUP + P], sh[:], ident_bf[:])
-            nc.vector.tensor_copy(out=nsv[:], in_=bank[:, 0:GROUP].rearrange("p (j r) -> p j r", j=COORDS)[:, :, 0:40])
-            nc.vector.tensor_copy(out=sh_t[:], in_=bank[:, GROUP : GROUP + P])
+            nc.scalar.copy(out=nsv[:], in_=bank[:, 0:GROUP].rearrange("p (j r) -> p j r", j=COORDS)[:, :, 0:40])
+            nc.scalar.copy(out=sh_t[:], in_=bank[:, GROUP : GROUP + P])
 
         a_bf = {}
 
@@ -112,7 +122,7 @@ def tile_blendshape_face_rig_d2_kernel(tc, A_bytes, A_scale, D_bytes, D_scale, n
                 a_bf[pair] = keep.tile([P, 2, K], BF16, name="a_bf%d" % pair)
             for j in range(K // SCALE_BLOCK):
                 cols = slice(SCALE_BLOCK * j, SCALE_BLOCK * (j + 1))
-                src = a_by[pair][:, ii, cols].bitcast(F8)
+                src = a_by[i][:, cols].bitcast(F8)
                 dst = a_bf[pair][:, ii, cols]
                 if j in S_A:
                     nc.scalar.activation(out=dst, in_=src, func=COPY, scale=a_sc[:, i, j : j + 1])
@@ -231,9 +241,11 @@ def tile_blendshape_face_rig_d2_kernel(tc, A_bytes, A_scale, D_bytes, D_scale, n
 
         for i in range(HALF):
             a_widen(i)
+        dummies(5)
         for pair in (0, 1):
             for g in range(PASSES):
                 a_turn(pair, g)
+        dummies(11)
         d_widen(0, 0, 0)
         a_out(0, 0, VC)
         a_out(0, 1, VC)
@@ -251,9 +263,9 @@ def tile_blendshape_face_rig_d2_kernel(tc, A_bytes, A_scale, D_bytes, D_scale, n
         a_turn(2, 0)
         a_turn(2, 1)
         d_quant(0)
-        small_turns()
         d_widen(1, 0, 0)
         d_widen(1, 0, 1)
+        small_turns()
         product(0, 0)
         d_inter(1, 0)
         a_turn(3, 0)
@@ -263,12 +275,12 @@ def tile_blendshape_face_rig_d2_kernel(tc, A_bytes, A_scale, D_bytes, D_scale, n
         d_quant(1)
         a_out(2, 1, SC)
         a_out(3, 0, VC)
+        a_out(3, 1, SC)
         product(0, 1)
         d_inter(2, 0)
         d_inter(2, 1)
         a_quant(1, 0)
         d_quant(2)
-        a_out(3, 1, SC)
         d_widen(1, 1, 0)
         d_widen(1, 1, 1)
         product(0, 2)

@@ -24,9 +24,10 @@ TILES = FRAMES // P
 HALF = TILES // 2
 GROUP = P * COORDS
 GROUPS = COLS // GROUP
+PREPS = ((1, 1, 1, 2), (1, 1, 1, 1))
 W_LEAD, P_LEAD = 2, 4
 V_WIDEN = (1, 9, 11, 14, 17, 19, 22, 25, 27, 30)
-S_OUT, S_OUT_UNITS = (3,), 11
+S_OUT, S_OUT_UNITS = (0,), 11
 S_A = (2, 5, 7)
 
 
@@ -82,21 +83,16 @@ def tile_blendshape_face_rig_d2_kernel(tc, A_bytes, A_scale, D_bytes, D_scale, n
             nc.scalar.dma_start(out=d_sc[32 * q : 32 * q + 32, :, :], in_=d_sc_view[q].partition_broadcast(32))
         stb = keep.tile([P, P], BF16, name="stb")
         nc.scalar.dma_start(out=stb[32:40, :], in_=strength.rearrange("(r v) -> r v", r=8))
-        nb = keep.tile([8, GROUP], BF16, name="nb")
-        nc.scalar.dma_start(out=nb[:], in_=neutral.rearrange("(r v) c -> r (v c)", r=8))
-        shb = keep.tile([P, TILES * COORDS], BF16, name="shb")
-        nc.scalar.dma_start(out=shb[:], in_=shift.rearrange("(p i) c -> p (i c)", i=TILES))
+        ns = keep.tile([P, GROUP], BF16, name="ns")
+        nc.vector.memset(ns[:], 0.0)
+        sh = keep.tile([P, P], BF16, name="sh")
+        nc.vector.memset(sh[:], 0.0)
+        nc.scalar.dma_start(out=ns[0:8, :], in_=neutral.rearrange("(r v) c -> r (v c)", r=8))
+        nc.scalar.dma_start(out=sh[:, 0 : TILES * COORDS], in_=shift.rearrange("(p i) c -> p (i c)", i=TILES))
         ident = keep.tile([P, P], F32, name="ident")
         make_identity(nc, ident[:])
-        ns = keep.tile([P, GROUP], BF16, name="ns")
-        nc.gpsimd.memset(ns[:], 0.0)
-        sh = keep.tile([P, P], BF16, name="sh")
-        nc.gpsimd.memset(sh[:], 0.0)
         ident_bf = keep.tile([P, P], BF16, name="ident_bf")
-        make_identity(nc, ident_bf[:])
-        nc.gpsimd.tensor_copy(out=ns[0:8, :], in_=nb[:])
-        nc.gpsimd.tensor_copy(out=sh[:, 0 : TILES * COORDS], in_=shb[:])
-        nc.gpsimd.tensor_copy(out=ns[32:40, :].rearrange("p (v c) -> p v c", c=COORDS), in_=stb[32:40, :].unsqueeze(2).to_broadcast([8, P, COORDS]))
+        nc.vector.tensor_copy(out=ident_bf[:], in_=ident[:])
 
         a_codes = keep.tile([P, PASSES, FRAMES], U32, name="a_codes", align_bytes=64)
         a_scales = keep.tile([P, PASSES, FRAMES], U8, name="a_scales", align_bytes=64)
@@ -176,6 +172,7 @@ def tile_blendshape_face_rig_d2_kernel(tc, A_bytes, A_scale, D_bytes, D_scale, n
             nc.vector.quantize_mx(out=d_codes[:, jt, :].bitcast(FP8X4), scales=d_scales[:, jt, :], in_=d_il[jt][:])
 
         x = {}
+        made = {}
 
         def product(u, j):
             s, h = divmod(u, 2)
@@ -190,6 +187,11 @@ def tile_blendshape_face_rig_d2_kernel(tc, A_bytes, A_scale, D_bytes, D_scale, n
                     rhs=a_codes[:, g, f].bitcast(FP8X4), rhs_scale=a_scales[:, g, f],
                     start=(g == 0), stop=(g == PASSES - 1),
                 )
+            made[u, j] = bank
+
+        def scaled(u, j):
+            s = u // 2
+            bank = made[u, j]
             x[u, j] = work.tile([P, 512], F32, name="x", bufs=8)
             nc.scalar.activation(out=x[u, j][:], in_=bank[:], func=IDENTITY, scale=nsv[:, j, 32 + s : 33 + s], bias=nsv[:, j, s : s + 1])
 
@@ -247,6 +249,7 @@ def tile_blendshape_face_rig_d2_kernel(tc, A_bytes, A_scale, D_bytes, D_scale, n
                 a_turn(pair, g)
         dummies(11)
         d_widen(0, 0, 0)
+        SC(out=ns[32:40, :].rearrange("p (v c) -> p v c", c=COORDS), in_=stb[32:40, :].unsqueeze(2).to_broadcast([8, P, COORDS]))
         a_out(0, 0, VC)
         a_out(0, 1, VC)
         d_widen(0, 0, 1)
@@ -267,6 +270,7 @@ def tile_blendshape_face_rig_d2_kernel(tc, A_bytes, A_scale, D_bytes, D_scale, n
         d_widen(1, 0, 1)
         small_turns()
         product(0, 0)
+        scaled(0, 0)
         d_inter(1, 0)
         a_turn(3, 0)
         a_turn(3, 1)
@@ -277,6 +281,7 @@ def tile_blendshape_face_rig_d2_kernel(tc, A_bytes, A_scale, D_bytes, D_scale, n
         a_out(3, 0, VC)
         a_out(3, 1, SC)
         product(0, 1)
+        scaled(0, 1)
         d_inter(2, 0)
         d_inter(2, 1)
         a_quant(1, 0)
@@ -284,6 +289,7 @@ def tile_blendshape_face_rig_d2_kernel(tc, A_bytes, A_scale, D_bytes, D_scale, n
         d_widen(1, 1, 0)
         d_widen(1, 1, 1)
         product(0, 2)
+        scaled(0, 2)
         a_quant(1, 1)
 
         widens = [(s, g, part) for s in range(2, GROUPS) for g in range(PASSES) for part in range(2)]
@@ -291,9 +297,9 @@ def tile_blendshape_face_rig_d2_kernel(tc, A_bytes, A_scale, D_bytes, D_scale, n
         last = None
         for jt in range(COORDS, COLS // P):
             preps.append((d_inter, (jt, 0)))
+            preps.append((d_inter, (jt, 1)))
             if last is not None:
                 preps.append((d_quant, (last,)))
-            preps.append((d_inter, (jt, 1)))
             last = jt
         preps.append((d_quant, (last,)))
 
@@ -318,12 +324,17 @@ def tile_blendshape_face_rig_d2_kernel(tc, A_bytes, A_scale, D_bytes, D_scale, n
             for step in range(4):
                 if 0 < u < units and step < COORDS:
                     product(u, step)
-                if step in (0, 2):
-                    widen_next(1)
-                if step == 3 and u >= 1:
-                    for ii in range(4):
-                        turn(u - 1, ii)
             for step in range(4):
                 if u >= 1:
+                    turn(u - 1, step)
+            for step in range(COORDS):
+                if 0 < u < units:
+                    scaled(u, step)
+                if step == 1 and u >= 1 and 0 in s_out(u - 1):
+                    shifted(u - 1, 0, u == units)
+                if step in (1, 2):
+                    widen_next(1)
+            for step in range(4):
+                if u >= 1 and step not in s_out(u - 1):
                     shifted(u - 1, step, u == units)
-                prep_next(2 if step == 0 and u % 2 == 0 else 1)
+                prep_next(PREPS[u % 2][step])

from contextlib import ExitStack

import concourse.mybir as mybir
from concourse.masks import make_identity

FRAMES, K, VERTS, COORDS, SCALE_BLOCK = 1024, 1024, 1024, 3, 128
COLS = VERTS * COORDS
FLOPS = 2 * FRAMES * K * COLS

F32 = mybir.dt.float32
BF16 = mybir.dt.bfloat16
U32 = mybir.dt.uint32
U8 = mybir.dt.uint8
F8 = mybir.dt.float8_e4m3fn
FP8X4 = mybir.dt.float8_e4m3fn_x4
MULT = mybir.AluOpType.mult
ADD = mybir.AluOpType.add
COPY = mybir.ActivationFunctionType.Copy
IDENTITY = mybir.ActivationFunctionType.Identity

P = 128
PASSES = K // 512
TILES = FRAMES // P
HALF = TILES // 2
GROUP = P * COORDS
GROUPS = COLS // GROUP
PREPS = ((1, 1, 1, 2), (1, 1, 1, 1))
W_LEAD, P_LEAD = 2, 4
V_WIDEN = (1, 9, 11, 14, 17, 19, 22, 25, 27, 30)
S_OUT, S_OUT_UNITS = (0,), 11
S_A = (2, 5, 7)


def tile_blendshape_face_rig_d2_kernel(tc, A_bytes, A_scale, D_bytes, D_scale, neutral, strength, shift, out):
    nc = tc.nc
    VC, SC = nc.vector.tensor_copy, nc.scalar.copy
    with ExitStack() as ctx:
        keep = ctx.enter_context(tc.tile_pool(name="keep", bufs=1))
        work = ctx.enter_context(tc.tile_pool(name="work", bufs=4))
        psum = ctx.enter_context(tc.psum_pool(name="psum", bufs=4))
        ctx.enter_context(tc.manual_schedule())

        warm = keep.tile([P, 512], BF16, name="warm")
        nc.vector.memset(warm[:], 0.0)

        def dummies(n):
            bank = psum.tile([P, 512], F32, name="mx")
            for again in range(n):
                nc.tensor.matmul(bank[:], lhsT=warm[:, 0:P], rhs=warm[:], start=True, stop=True)

        a_sc = keep.tile([P, TILES, K // SCALE_BLOCK], F32, name="a_sc")
        nc.sync.dma_start(out=a_sc[:], in_=A_scale.rearrange("(p i) j -> p i j", i=TILES))
        a_view = A_bytes.rearrange("(p i) k -> p i k", i=TILES)
        d_view = D_bytes.rearrange("(g p t) n -> g p t n", p=P, t=4)
        a_by = []
        d_by = {}

        def load_a(first, count):
            t = keep.tile([P, count, K], U8, name="a_by%d" % first)
            nc.sync.dma_start(out=t[:], in_=a_view[:, first : first + count, :])
            for i in range(count):
                a_by.append(t[:, i, :])

        def load_d(s, g):
            t = keep.tile([P, 4, GROUP], U8, name="d_by%d_%d" % (s, g))
            nc.sync.dma_start(out=t[:], in_=d_view[g][:, :, s * GROUP : (s + 1) * GROUP])
            d_by[s, g] = t

        load_a(0, 1)
        load_a(1, 1)
        load_a(2, 2)
        for g in range(PASSES):
            load_d(0, g)
        load_a(4, 2)
        load_a(6, 2)
        for s in range(1, GROUPS):
            for g in range(PASSES):
                load_d(s, g)

        d_sc = keep.tile([P, PASSES, COLS // SCALE_BLOCK], F32, name="d_sc")
        d_sc_view = D_scale.rearrange("(g q) j -> q g j", q=4)
        for q in range(4):
            nc.scalar.dma_start(out=d_sc[32 * q : 32 * q + 32, :, :], in_=d_sc_view[q].partition_broadcast(32))
        stb = keep.tile([P, P], BF16, name="stb")
        nc.scalar.dma_start(out=stb[32:40, :], in_=strength.rearrange("(r v) -> r v", r=8))
        ns = keep.tile([P, GROUP], BF16, name="ns")
        nc.vector.memset(ns[:], 0.0)
        sh = keep.tile([P, P], BF16, name="sh")
        nc.vector.memset(sh[:], 0.0)
        nc.scalar.dma_start(out=ns[0:8, :], in_=neutral.rearrange("(r v) c -> r (v c)", r=8))
        nc.scalar.dma_start(out=sh[:, 0 : TILES * COORDS], in_=shift.rearrange("(p i) c -> p (i c)", i=TILES))
        ident = keep.tile([P, P], F32, name="ident")
        make_identity(nc, ident[:])
        ident_bf = keep.tile([P, P], BF16, name="ident_bf")
        nc.vector.tensor_copy(out=ident_bf[:], in_=ident[:])

        a_codes = keep.tile([P, PASSES, FRAMES], U32, name="a_codes", align_bytes=64)
        a_scales = keep.tile([P, PASSES, FRAMES], U8, name="a_scales", align_bytes=64)
        d_codes = keep.tile([P, COLS // P, PASSES * P], U32, name="d_codes", align_bytes=64)
        d_scales = keep.tile([P, COLS // P, PASSES * P], U8, name="d_scales", align_bytes=64)

        sh_t = keep.tile([P, P], BF16, name="sh_t")
        nsv = keep.tile([P, COORDS, 40], F32, name="nsv")

        def small_turns():
            bank = psum.tile([P, 1024], BF16, name="tr")
            for j in range(COORDS):
                nc.tensor.transpose(bank[:, P * j : P * (j + 1)], ns[:, P * j : P * (j + 1)], ident_bf[:])
            nc.tensor.transpose(bank[:, GROUP : GROUP + P], sh[:], ident_bf[:])
            nc.scalar.copy(out=nsv[:], in_=bank[:, 0:GROUP].rearrange("p (j r) -> p j r", j=COORDS)[:, :, 0:40])
            nc.scalar.copy(out=sh_t[:], in_=bank[:, GROUP : GROUP + P])

        a_bf = {}

        def a_widen(i):
            pair, ii = divmod(i, 2)
            if ii == 0:
                a_bf[pair] = keep.tile([P, 2, K], BF16, name="a_bf%d" % pair)
            for j in range(K // SCALE_BLOCK):
                cols = slice(SCALE_BLOCK * j, SCALE_BLOCK * (j + 1))
                src = a_by[i][:, cols].bitcast(F8)
                dst = a_bf[pair][:, ii, cols]
                if j in S_A:
                    nc.scalar.activation(out=dst, in_=src, func=COPY, scale=a_sc[:, i, j : j + 1])
                else:
                    nc.vector.tensor_scalar(out=dst, in0=src, scalar1=a_sc[:, i, j : j + 1], scalar2=None, op0=MULT)

        a_grp = {}

        a_bank = {}

        def a_turn(pair, g):
            bank = psum.tile([P, 512], F32, name="tr")
            for ii in range(2):
                words = a_bf[pair][:, ii, :].bitcast(F32)
                for u in range(2):
                    at = 256 * ii + 128 * u
                    nc.tensor.transpose(bank[:, at : at + 128], words[:, 256 * g + u : 256 * (g + 1) : 2], ident[:])
            a_bank[pair, g] = bank

        def a_out(pair, g, copy):
            h, part = divmod(pair, 2)
            bank = a_bank[pair, g]
            if part == 0:
                a_grp[h, g] = work.tile([P, HALF * P * 4], BF16, name="a_grp", align_bytes=64)
            dst = a_grp[h, g][:].bitcast(F32)[:, 512 * part : 512 * (part + 1)].rearrange("p (i r u) -> p i r u", i=2, u=2)
            copy(out=dst, in_=bank[:].rearrange("p (i u r) -> p i r u", i=2, u=2))

        def a_quant(h, g):
            f = slice(512 * h, 512 * (h + 1))
            nc.vector.quantize_mx(out=a_codes[:, g, f].bitcast(FP8X4), scales=a_scales[:, g, f], in_=a_grp[h, g][:])

        d_wd = {}
        d_il = {}

        def d_widen(s, g, part):
            if part == 0:
                d_wd[s, g] = work.tile([P, 4 * GROUP], BF16, name="d_wd", bufs=6)
            cols = slice(768 * part, 768 * (part + 1))
            copy = VC if (4 * s + 2 * g + part) % 32 in V_WIDEN else SC
            copy(out=d_wd[s, g][:, cols], in_=d_by[s, g][:].rearrange("p t n -> p (t n)")[:, cols].bitcast(F8))

        def d_inter(jt, g):
            s, j = divmod(jt, COORDS)
            if g == 0:
                d_il[jt] = work.tile([P, PASSES * P * 4], BF16, name="d_il", align_bytes=64)
            src = d_wd[s, g][:].rearrange("p (t n) -> p t n", t=4)[:, :, P * j : P * (j + 1)].rearrange("p t (n i) -> p n t i", i=4)
            dst = d_il[jt][:, 512 * g : 512 * (g + 1)].rearrange("p (n i t) -> p n t i", i=4, t=4)
            nc.vector.tensor_scalar(out=dst, in0=src, scalar1=d_sc[:, g, jt : jt + 1], scalar2=None, op0=MULT)

        def d_quant(jt):
            nc.vector.quantize_mx(out=d_codes[:, jt, :].bitcast(FP8X4), scales=d_scales[:, jt, :], in_=d_il[jt][:])

        x = {}
        made = {}

        def product(u, j):
            s, h = divmod(u, 2)
            jt = COORDS * s + j
            f = slice(512 * h, 512 * (h + 1))
            bank = psum.tile([P, 512], F32, name="mx")
            for g in range(PASSES):
                c = slice(P * g, P * (g + 1))
                nc.tensor.matmul_mx(
                    out=bank[:],
                    lhsT=d_codes[:, jt, c].bitcast(FP8X4), lhsT_scale=d_scales[:, jt, c],
                    rhs=a_codes[:, g, f].bitcast(FP8X4), rhs_scale=a_scales[:, g, f],
                    start=(g == 0), stop=(g == PASSES - 1),
                )
            made[u, j] = bank

        def scaled(u, j):
            s = u // 2
            bank = made[u, j]
            x[u, j] = work.tile([P, 512], F32, name="x", bufs=8)
            nc.scalar.activation(out=x[u, j][:], in_=bank[:], func=IDENTITY, scale=nsv[:, j, 32 + s : 33 + s], bias=nsv[:, j, s : s + 1])

        turned = {}

        def s_out(u):
            return S_OUT if u < S_OUT_UNITS else ()

        def turn(u, ii):
            bank = psum.tile([P, 512], F32, name="tr")
            i = HALF * (u % 2) + ii
            if ii in s_out(u):
                nc.tensor.matmul(
                    bank[:, 0:GROUP].rearrange("p (v c) -> p v c", c=COORDS), lhsT=sh_t[:],
                    rhs=ident_bf[:, COORDS * i : COORDS * (i + 1)].unsqueeze(1).to_broadcast([P, P, COORDS]),
                    start=True, stop=False,
                )
            for j in range(COORDS):
                block, src = bank[:, P * j : P * (j + 1)], x[u, j][:, P * ii : P * (ii + 1)]
                if ii in s_out(u):
                    nc.tensor.matmul(block, lhsT=src, rhs=ident[:], start=False, stop=(j == COORDS - 1), is_transpose=True)
                else:
                    nc.tensor.transpose(block, src, ident[:])
            turned[u, ii] = bank

        out_view = out.rearrange("(p i) v c -> p i (v c)", i=TILES)
        o = {}

        def shifted(u, ii, single):
            s, h = divmod(u, 2)
            i = HALF * h + ii
            if ii % 2 == 0:
                o[u, ii // 2] = work.tile([P, 2, GROUP], F32, name="o", bufs=6)
            t = o[u, ii // 2]
            if ii in s_out(u):
                nc.scalar.copy(out=t[:, ii % 2, :], in_=turned[u, ii][:, 0:GROUP])
            else:
              nc.vector.tensor_tensor(
                out=t[:, ii % 2, :].rearrange("p (v c) -> p v c", c=COORDS),
                in0=turned[u, ii][:, 0:GROUP].rearrange("p (v c) -> p v c", c=COORDS),
                in1=sh[:, COORDS * i : COORDS * (i + 1)].unsqueeze(1).to_broadcast([P, P, COORDS]),
                op=ADD,
            )
            cols = slice(GROUP * s, GROUP * (s + 1))
            if single:
                nc.sync.dma_start(out=out_view[:, i, cols], in_=t[:, ii % 2, :])
            elif ii % 2 == 1:
                nc.sync.dma_start(out=out_view[:, i - 1 : i + 1, cols], in_=t[:])

        for i in range(HALF):
            a_widen(i)
        dummies(5)
        for pair in (0, 1):
            for g in range(PASSES):
                a_turn(pair, g)
        dummies(11)
        d_widen(0, 0, 0)
        SC(out=ns[32:40, :].rearrange("p (v c) -> p v c", c=COORDS), in_=stb[32:40, :].unsqueeze(2).to_broadcast([8, P, COORDS]))
        a_out(0, 0, VC)
        a_out(0, 1, VC)
        d_widen(0, 0, 1)
        a_out(1, 0, VC)
        a_out(1, 1, SC)
        d_inter(0, 0)
        a_quant(0, 0)
        for part in range(2):
            d_widen(0, 1, part)
        a_quant(0, 1)
        d_inter(0, 1)
        for i in range(HALF, TILES):
            a_widen(i)
        a_turn(2, 0)
        a_turn(2, 1)
        d_quant(0)
        d_widen(1, 0, 0)
        d_widen(1, 0, 1)
        small_turns()
        product(0, 0)
        scaled(0, 0)
        d_inter(1, 0)
        a_turn(3, 0)
        a_turn(3, 1)
        d_inter(1, 1)
        a_out(2, 0, VC)
        d_quant(1)
        a_out(2, 1, SC)
        a_out(3, 0, VC)
        a_out(3, 1, SC)
        product(0, 1)
        scaled(0, 1)
        d_inter(2, 0)
        d_inter(2, 1)
        a_quant(1, 0)
        d_quant(2)
        d_widen(1, 1, 0)
        d_widen(1, 1, 1)
        product(0, 2)
        scaled(0, 2)
        a_quant(1, 1)

        widens = [(s, g, part) for s in range(2, GROUPS) for g in range(PASSES) for part in range(2)]
        preps = []
        last = None
        for jt in range(COORDS, COLS // P):
            preps.append((d_inter, (jt, 0)))
            preps.append((d_inter, (jt, 1)))
            if last is not None:
                preps.append((d_quant, (last,)))
            last = jt
        preps.append((d_quant, (last,)))

        def widen_next(n):
            for w in widens[:n]:
                d_widen(*w)
            rest = widens[n:]
            widens.clear()
            widens.extend(rest)

        def prep_next(n):
            for f, args in preps[:n]:
                f(*args)
            rest = preps[n:]
            preps.clear()
            preps.extend(rest)

        units = 2 * GROUPS
        widen_next(W_LEAD)
        prep_next(P_LEAD)
        for u in range(units + 1):
            for step in range(4):
                if 0 < u < units and step < COORDS:
                    product(u, step)
            for step in range(4):
                if u >= 1:
                    turn(u - 1, step)
            for step in range(COORDS):
                if 0 < u < units:
                    scaled(u, step)
                if step == 1 and u >= 1 and 0 in s_out(u - 1):
                    shifted(u - 1, 0, u == units)
                if step in (1, 2):
                    widen_next(1)
            for step in range(4):
                if u >= 1 and step not in s_out(u - 1):
                    shifted(u - 1, step, u == units)
                prep_next(PREPS[u % 2][step])
